import numpy as np
import ml_dtypes


def mxq(x, axis, fmt="e4m3"):
    dtype, down = {"e4m3": (ml_dtypes.float8_e4m3fn, 7), "e5m2": (ml_dtypes.float8_e5m2, 14)}[fmt]
    v = np.moveaxis(np.asarray(x, np.float32).astype(ml_dtypes.bfloat16).astype(np.float64), axis, -1)
    blocks = v.reshape(v.shape[:-1] + (-1, 32))
    amax = np.abs(blocks).max(-1, keepdims=True)
    byte = np.maximum(np.where(amax > 0, np.frexp(amax)[1] - 1 + 127, 0) - down, 1)
    scale = np.exp2(byte - 127.0)
    codes = (blocks / scale).astype(np.float32).astype(dtype).astype(np.float64)
    return np.moveaxis((codes * scale).reshape(v.shape), -1, axis)


WIDE = False


def mx_kscale(k):
    if not WIDE:
        return np.ones(k)
    levels = np.array([10, -10, 5, -5, 0])
    if k % 512:
        return np.exp2(np.random.permutation(np.resize(levels, k // 32))).repeat(32)
    a = np.empty((k // 512, 16))
    for p in range(k // 512):
        a[p, :8] = np.random.permutation(np.resize(levels, 8))
        for g in range(8):
            far = levels[np.abs(levels - a[p, g]) >= 10]
            a[p, g + 8] = far[np.random.randint(len(far))]
    return np.exp2(a.ravel()).repeat(32)


def f64(x):
    return np.asarray(x).astype(np.float64)


def striped(idx):
    return np.tile(np.asarray(idx).reshape(-1, 16).T, (8, 1)).astype(np.uint16)


def unstriped(offs):
    return offs[:16].T.reshape(-1).astype(np.int64)


E2M1 = np.array([0.0, 0.5, 1.0, 1.5, 2.0, 3.0, 4.0, 6.0, -0.0, -0.5, -1.0, -1.5, -2.0, -3.0, -4.0, -6.0])


def pack_weight(w, fmt):
    k, n = w.shape
    w = f64(np.asarray(w, np.float32).astype(ml_dtypes.bfloat16)).reshape(k // 32, 32, n)
    amax = np.abs(w).max(1)
    if fmt == "e4m3":
        byte = np.frexp(amax)[1] - 1 + 127 - 7
    else:
        mant, ex = np.frexp(amax / 6.0)
        byte = np.where(mant > 0.5, ex, ex - 1) + 127
    byte = np.clip(np.where(amax > 0, byte, 1), 1, 254)
    scaled = (w * np.exp2(127.0 - byte)[:, None, :]).reshape(k, n).astype(np.float32)
    by_word = np.ascontiguousarray(scaled.reshape(k // 512, 128, 4, n).transpose(0, 1, 3, 2))
    if fmt == "e4m3":
        words = by_word.astype(ml_dtypes.float8_e4m3fn).view(np.uint8)
    else:
        c = by_word.astype(ml_dtypes.float4_e2m1fn).view(np.uint8) & 0xF
        words = (c[..., 0::2] | (c[..., 1::2] << 4)).reshape(k // 512, 128, 2 * n)
    return np.ascontiguousarray(words), np.ascontiguousarray(byte.astype(np.uint8).reshape(k // 512, 16, n))


def unpack_weight(words, scales, fmt):
    g, _, n = scales.shape
    words = np.ascontiguousarray(words).reshape(g, 128, n, -1)
    if fmt == "e4m3":
        vals = words.view(ml_dtypes.float8_e4m3fn).astype(np.float64)
    else:
        nib = np.empty((g, 128, n, 4), np.uint8)
        nib[..., 0::2] = words & 0xF
        nib[..., 1::2] = words >> 4
        vals = E2M1[nib]
    vals = vals * np.repeat(np.exp2(scales.astype(np.float64) - 127.0), 8, axis=1)[..., None]
    return vals.transpose(0, 1, 3, 2).reshape(g * 512, n)


def softplus(v):
    return np.log(1.0 + np.exp(v))


def sigmoid(v):
    return 1.0 / (1.0 + np.exp(-v))


D, E, T, I, G, U, Q = 512, 512, 4096, 1024, 64, 512, 128


def setup_inputs():
    n = np.random.standard_normal
    idx = np.random.permutation(T)[:I]
    idx2 = np.random.permutation(U)[:G]
    fd = mx_kscale(D)
    fe = mx_kscale(E)
    keysp = pack_weight(n((D, T)) / fd[:, None], "e4m3")
    valsp = pack_weight(n((E, T)) / fe[:, None], "e4m3")
    return {
        "query": (n((D, Q)) * 1.0 / np.sqrt(D) * fd[:, None]).astype(np.float32),
        "keys_words": keysp[0],
        "keys_scales": keysp[1],
        "ptab": (n((Q, U)) * 0.5).astype(np.float32),
        "reserve": (np.random.uniform(50.0, 200.0, (Q, 1))).astype(np.float32),
        "gout": (n((E, Q)) * 1 / np.sqrt(E) * fe[:, None]).astype(np.float32),
        "vals_words": valsp[0],
        "vals_scales": valsp[1],
        "lam": (np.random.uniform(0.5, 1.5, (Q, 1))).astype(np.float32),
        "dquery": (n((D, Q)) * 1.0 / np.sqrt(D) * fd[:, None]).astype(np.float32),
        "base": (0.5 * n((Q, G))).astype(np.float32),
        "offs": striped(idx),
        "offs2": striped(idx2),
    }


def reference(query, keys_words, keys_scales, ptab, reserve, gout, vals_words, vals_scales, lam, dquery, base, offs, offs2):
    idx = unstriped(offs)
    idx2 = unstriped(offs2)
    keysu = unpack_weight(keys_words, keys_scales, "e4m3")
    valsu = unpack_weight(vals_words, vals_scales, "e4m3")
    queryq = mxq(f64(query), 0, "e4m3")
    keysidxg = keysu[:, idx]
    a = queryq.T @ keysidxg
    dqueryq = mxq(f64(dquery), 0, "e4m3")
    ta = dqueryq.T @ keysidxg
    tp = f64(ptab)[:, idx2] * f64(lam)
    tr1 = np.repeat(tp, I // G, axis=1)
    p = softplus(a - tr1)
    z = np.sum(p, axis=1, keepdims=True) + f64(reserve)
    goutq = mxq(f64(gout), 0, "e4m3")
    valsidxg = valsu[:, idx]
    c0 = goutq.T @ valsidxg
    dz = np.sum(p * c0, axis=1, keepdims=True) / np.square(z) * (-1.0)
    dp = 1.0 / z * c0 + dz
    xp = ta * sigmoid(a - tr1)
    xz = np.sum(xp, axis=1, keepdims=True)
    xdz = (np.sum(xp * c0, axis=1, keepdims=True) - xz * z * 2.0 * np.sum(p * c0, axis=1, keepdims=True) / np.square(z)) / np.square(z) * (-1.0)
    xdp = xz * 1.0 / np.square(z) * (-1.0) * c0 + xdz
    xdtr1 = (xdp * sigmoid(a - tr1) + ta * sigmoid(a - tr1) * (1.0 - sigmoid(a - tr1)) * dp) * (-1.0)
    xdtp = xdtr1.reshape(Q, G, I // G).sum(axis=2)
    y = xdtp * 64.0 + f64(base)
    return y

@@ -1,0 +1,203 @@
+from contextlib import ExitStack
+
+import concourse.mybir as mybir
+from concourse.masks import make_identity
+
+F32 = mybir.dt.float32
+BF16 = mybir.dt.bfloat16
+I32 = mybir.dt.int32
+U32 = mybir.dt.uint32
+U16 = mybir.dt.uint16
+U8 = mybir.dt.uint8
+FP8X4 = mybir.dt.float8_e4m3fn_x4
+ALU = mybir.AluOpType
+ACT = mybir.ActivationFunctionType
+
+P = 128
+PACK = 4
+TOKENS = 4096
+SLOTS = 1024
+PAGES = 64
+PAGE = 16
+TABLE = 512
+BANK = 512
+HALVES = SLOTS // BANK
+HALF_PAGES = PAGES // HALVES
+VALS_ROW = 4
+LN_FLOOR = 2.0 ** -40
+GAIN = 64.0
+
+FLOPS = 3 * 2 * 512 * P * SLOTS
+
+
+def tile_attend_hvpagefloor_kernel(tc, query, keys_words, keys_scales, ptab, reserve, gout, vals_words, vals_scales,
+                                    lam, dquery, base, offs, offs2, out):
+    nc = tc.nc
+    with ExitStack() as ctx:
+        sb = ctx.enter_context(tc.tile_pool(name="sb", bufs=1))
+        ps = ctx.enter_context(tc.psum_pool(name="ps", bufs=1))
+
+        slots = sb.tile([P, SLOTS // 16], U16, name="slots")
+        pages = sb.tile([P, PAGES // 16], U16, name="pages")
+        nc.sync.dma_start(slots[:], offs)
+
+        def load_scales(name, src, row, queue):
+            window = sb.tile([P, TOKENS], U8, name=name, align_bytes=64)
+            nc.vector.memset(window[:].bitcast(I32), 0)
+            for quad in range(4):
+                queue.dma_start(window[32 * quad + row:32 * quad + row + 4, :].bitcast(I32),
+                                src[0, 4 * quad:4 * quad + 4, :].bitcast(I32))
+            return window
+
+        def load_words(name, src, tag):
+            window = sb.tile([P, TOKENS], I32, name=name, tag=tag, align_bytes=64)
+            nc.sync.dma_start(window[:], src[0].rearrange("p n t -> p (n t)").bitcast(I32))
+            return window
+
+        def load_rows(name, src, tag, queue):
+            raw = sb.tile([P, PACK, P], F32, name=name, tag=tag, align_bytes=64)
+            queue.dma_start(raw[:], src.rearrange("(p j) w -> p j w", j=PACK))
+            return raw
+
+        def load_plain(name, src, width, tag, queue):
+            tile = sb.tile([P, width], F32, name=name, tag=tag, align_bytes=64)
+            queue.dma_start(tile[:], src)
+            return tile
+
+        nc.sync.dma_start(pages[:], offs2)
+        q_raw = load_rows("q_raw", query, "stage_a", nc.sync)
+        key_pool = load_words("key_pool", keys_words, "key_pool")
+        dq_raw = load_rows("dq_raw", dquery, "stage_b", nc.gpsimd)
+        lam_col = load_plain("lam_col", lam, 1, "col", nc.gpsimd)
+        key_scale_pool = load_scales("key_scale_pool", keys_scales, 0, nc.scalar)
+        val_scale_pool = load_scales("val_scale_pool", vals_scales, VALS_ROW, nc.gpsimd)
+
+        ident = sb.tile([P, P], F32, name="ident")
+        make_identity(nc, ident[:])
+        ln_floor = sb.tile([P, 1], F32, name="ln_floor")
+        nc.gpsimd.memset(ln_floor[:], LN_FLOOR)
+
+        def quantise(name, raws):
+            width = P * len(raws)
+            grouped = sb.tile([P, width, PACK], BF16, name=name + "_bf16", align_bytes=64)
+            for n, raw in enumerate(raws):
+                nc.scalar.copy(grouped[:, n * P:(n + 1) * P, :], raw[:].rearrange("p j w -> p w j"))
+            codes = sb.tile([P, width], U32, name=name + "_codes", align_bytes=64)
+            scales = sb.tile([P, width], U8, name=name + "_scales", align_bytes=64)
+            nc.vector.quantize_mx(out=codes[:].bitcast(FP8X4), scales=scales[:],
+                                  in_=grouped[:].rearrange("p w j -> p (w j)"))
+            return codes, scales
+
+        def gather_scales(name, window):
+            picked = sb.tile([P, SLOTS], U8, name=name, align_bytes=64)
+            nc.vector.tensor_copy(picked[:], window[:].indirect(slots[:]))
+            return picked
+
+        def gather_words(name, window, half):
+            picked = sb.tile([P, BANK], U32, name=name, align_bytes=64)
+            cols = BANK // 16
+            nc.vector.tensor_copy(picked[:], window[:].bitcast(U32).indirect(slots[:, half * cols:(half + 1) * cols]))
+            return picked
+
+        def product(tag, codes, scales, col, words, word_scales, row, half):
+            bank = ps.tile([P, BANK], F32, name=tag, tag=tag)
+            nc.tensor.matmul_mx(out=bank[:], lhsT=codes[:, col:col + P].bitcast(FP8X4), lhsT_scale=scales[:, col:col + P],
+                                rhs=words[:].bitcast(FP8X4), rhs_scale=word_scales[row:P, half * BANK:(half + 1) * BANK],
+                                start=True, stop=True)
+            return bank[:].rearrange("p (g r) -> p r g", r=PAGE)
+
+        key_scales = gather_scales("key_scales", key_scale_pool)
+        val_scales = gather_scales("val_scales", val_scale_pool)
+        q_codes, q_scales = quantise("q", [q_raw, dq_raw])
+        table = load_plain("table", ptab, TABLE, "stage_a", nc.sync)
+        val_pool = load_words("val_pool", vals_words, "stage_b")
+        floors = sb.tile([P, PAGES], F32, name="floors", tag="floors", align_bytes=64)
+        nc.vector.tensor_copy(floors[:], table[:].indirect(pages[:]))
+        go_raw = load_rows("go_raw", gout, "stage_a", nc.sync)
+
+        score, dscore = [], []
+        for half in range(HALVES):
+            keys = gather_words("keys%d" % half, key_pool, half)
+            score.append(product("a%d" % half, q_codes, q_scales, 0, keys, key_scales, 0, half))
+            dscore.append(product("t%d" % half, q_codes, q_scales, P, keys, key_scales, 0, half))
+
+        def wide(name):
+            return sb.tile([P, PAGE, PAGES], F32, name=name)
+
+        def col(name, width=1):
+            return sb.tile([P, width], F32, name=name)
+
+        def part(half):
+            return slice(half * HALF_PAGES, (half + 1) * HALF_PAGES)
+
+        y, log_rest, neg_p, neg_xp, w = wide("y"), wide("log_rest"), wide("neg_p"), wide("neg_xp"), wide("w")
+        pair = sb.tile([P, PAGE, 2, PAGES], F32, name="pair")
+        rest, n_term = pair[:, :, 0, :], pair[:, :, 1, :]
+        neg_xz = [col("neg_xz%d" % h) for h in range(HALVES)]
+        for half in range(HALVES):
+            g = part(half)
+            nc.vector.scalar_tensor_tensor(y[:, :, g], floors[:, g].unsqueeze(1).to_broadcast([P, PAGE, HALF_PAGES]),
+                                           lam_col[:], score[half], ALU.mult, ALU.subtract)
+            nc.scalar.activation(rest[:, :, g], y[:, :, g], ACT.Sigmoid)
+        reserve_col = load_plain("reserve_col", reserve, 1, "col", nc.sync)
+        base_t = load_plain("base_t", base, PAGES, "floors", nc.sync)
+        for half in range(HALVES):
+            g = part(half)
+            nc.vector.scalar_tensor_tensor(neg_xp[:, :, g], rest[:, :, g], 1.0, dscore[half], ALU.subtract, ALU.mult,
+                                           accum_out=neg_xz[half][:])
+        nc.scalar.activation(log_rest[:], rest, ACT.Ln, bias=ln_floor[:])
+
+        go_codes, go_scales = quantise("go", [go_raw])
+        c0 = []
+        for half in range(HALVES):
+            vals = gather_words("vals%d" % half, val_pool, half)
+            c0.append(product("c%d" % half, go_codes, go_scales, 0, vals, val_scales, VALS_ROW, half))
+
+        neg_sum_p, z, inv_z, alpha, c1, c2 = (col(n) for n in ("neg_sum_p", "z", "inv_z", "alpha", "c1", "c2"))
+        nc.vector.scalar_tensor_tensor(neg_p[:], y[:], 1.0, log_rest[:], ALU.mult, ALU.min, accum_out=neg_sum_p[:])
+        nc.vector.tensor_tensor(z[:], reserve_col[:], neg_sum_p[:], ALU.subtract)
+        nc.vector.reciprocal(inv_z[:], z[:])
+        nc.vector.tensor_scalar(alpha[:], neg_xz[0][:], neg_xz[1][:], inv_z[:], ALU.add, ALU.mult)
+        nc.scalar.activation(c1[:], inv_z[:], ACT.Square, scale=8.0)
+        nc.scalar.activation(c2[:], inv_z[:], ACT.Copy, scale=GAIN)
+        nc.vector.scalar_tensor_tensor(n_term, neg_xp[:], alpha[:], rest, ALU.add, ALU.mult)
+
+        def page_sums(name, blocks, tags):
+            turned = ps.tile([P, P], F32, name=name + "_turned", tag=tags[0])
+            for n, block in enumerate(blocks):
+                nc.tensor.matmul(turned[:], lhsT=block, rhs=ident[:], is_transpose=True,
+                                 start=(n == 0), stop=(n == len(blocks) - 1))
+            staged = sb.tile([P, P], F32, name=name + "_staged")
+            nc.scalar.copy(staged[:], turned[:])
+            back = ps.tile([P, P], F32, name=name + "_back", tag=tags[1])
+            nc.tensor.transpose(back[:], staged[:], ident[:])
+            return back
+
+        for half in range(HALVES):
+            g = part(half)
+            nc.vector.scalar_tensor_tensor(w[:, :, g], n_term[:, :, g], alpha[:], c0[half], ALU.subtract, ALU.mult)
+        pair_sums = page_sums("pair", [pair[:, r, :, :].rearrange("p a g -> p (a g)") for r in range(PAGE)], ("f", "g"))
+        w_sums = page_sums("w", [w[:, r:r + 2, :].rearrange("p a g -> p (a g)") for r in range(0, PAGE, 2)], ("a0", "a1"))
+
+        e1, rest32, e2 = (col(n, PAGES) for n in ("e1", "rest32", "e2"))
+        nc.scalar.activation(e1[:], pair_sums[:, 0:PAGES], ACT.Copy, bias=-float(PAGE))
+        nc.scalar.activation(rest32[:], pair_sums[:, 0:PAGES], ACT.Copy, bias=-2.0 * PAGE)
+
+        dots = {}
+        for name, factor in (("b", neg_xp), ("a", neg_p)):
+            for half in range(HALVES):
+                g = part(half)
+                unused = sb.tile([P, PAGE, HALF_PAGES], F32, name="unused_%s%d" % (name, half))
+                dots[name, half] = col("dot_%s%d" % (name, half))
+                nc.vector.scalar_tensor_tensor(unused[:], factor[:, :, g], c1[:], c0[half], ALU.mult, ALU.mult,
+                                               accum_out=dots[name, half][:])
+
+        nc.vector.scalar_tensor_tensor(e2[:], rest32[:], alpha[:], pair_sums[:, PAGES:P], ALU.mult, ALU.add)
+        terms = [(e1[:], dots["b", 0]), (e1[:], dots["b", 1]), (w_sums[:, 0:PAGES], c2), (w_sums[:, PAGES:P], c2),
+                 (e2[:], dots["a", 0]), (e2[:], dots["a", 1])]
+        total = base_t
+        for n, (term, factor) in enumerate(terms):
+            nxt = col("total%d" % n, PAGES)
+            nc.vector.scalar_tensor_tensor(nxt[:], term, factor[:], total[:], ALU.mult, ALU.add)
+            total = nxt
+        nc.sync.dma_start(out, total[:])

@@ -65,23 +65,27 @@ def tile_attend_hvpagefloor_kernel(tc, query, keys_words, keys_scales, ptab, res
             return tile
 
         nc.sync.dma_start(pages[:], offs2)
-        q_raw = load_rows("q_raw", query, "stage_a", nc.sync)
-        key_pool = load_words("key_pool", keys_words, "key_pool")
-        dq_raw = load_rows("dq_raw", dquery, "stage_b", nc.gpsimd)
-        lam_col = load_plain("lam_col", lam, 1, "col", nc.gpsimd)
+        lam_col = load_plain("lam_col", lam, 1, "lam_col", nc.scalar)
         key_scale_pool = load_scales("key_scale_pool", keys_scales, 0, nc.scalar)
-        val_scale_pool = load_scales("val_scale_pool", vals_scales, VALS_ROW, nc.gpsimd)
+        val_scale_pool = load_scales("val_scale_pool", vals_scales, VALS_ROW, nc.scalar)
+        q_raw = load_rows("q_raw", query, "stage_a", nc.sync)
+        dq_raw = load_rows("dq_raw", dquery, "dq_raw", nc.sync)
+        table = load_plain("table", ptab, TABLE, "table", nc.sync)
+        key_pool = load_words("key_pool", keys_words, "key_pool")
+        val_pool = load_words("val_pool", vals_words, "val_pool")
+        reserve_col = load_plain("reserve_col", reserve, 1, "reserve_col", nc.sync)
+        base_t = load_plain("base_t", base, PAGES, "base_t", nc.sync)
 
         ident = sb.tile([P, P], F32, name="ident")
         make_identity(nc, ident[:])
         ln_floor = sb.tile([P, 1], F32, name="ln_floor")
         nc.gpsimd.memset(ln_floor[:], LN_FLOOR)
 
-        def quantise(name, raws):
+        def quantise(name, raws, copy):
             width = P * len(raws)
             grouped = sb.tile([P, width, PACK], BF16, name=name + "_bf16", align_bytes=64)
             for n, raw in enumerate(raws):
-                nc.scalar.copy(grouped[:, n * P:(n + 1) * P, :], raw[:].rearrange("p j w -> p w j"))
+                copy(grouped[:, n * P:(n + 1) * P, :], raw[:].rearrange("p j w -> p w j"))
             codes = sb.tile([P, width], U32, name=name + "_codes", align_bytes=64)
             scales = sb.tile([P, width], U8, name=name + "_scales", align_bytes=64)
             nc.vector.quantize_mx(out=codes[:].bitcast(FP8X4), scales=scales[:],
@@ -93,33 +97,35 @@ def tile_attend_hvpagefloor_kernel(tc, query, keys_words, keys_scales, ptab, res
             nc.vector.tensor_copy(picked[:], window[:].indirect(slots[:]))
             return picked
 
-        def gather_words(name, window, half):
-            picked = sb.tile([P, BANK], U32, name=name, align_bytes=64)
+        def gather_words(picked, window, half):
             cols = BANK // 16
-            nc.vector.tensor_copy(picked[:], window[:].bitcast(U32).indirect(slots[:, half * cols:(half + 1) * cols]))
-            return picked
+            words = picked[:, half * BANK:(half + 1) * BANK]
+            nc.vector.tensor_copy(words, window[:].bitcast(U32).indirect(slots[:, half * cols:(half + 1) * cols]))
+            return words
 
         def product(tag, codes, scales, col, words, word_scales, row, half):
             bank = ps.tile([P, BANK], F32, name=tag, tag=tag)
             nc.tensor.matmul_mx(out=bank[:], lhsT=codes[:, col:col + P].bitcast(FP8X4), lhsT_scale=scales[:, col:col + P],
-                                rhs=words[:].bitcast(FP8X4), rhs_scale=word_scales[row:P, half * BANK:(half + 1) * BANK],
+                                rhs=words.bitcast(FP8X4), rhs_scale=word_scales[row:P, half * BANK:(half + 1) * BANK],
                                 start=True, stop=True)
             return bank[:].rearrange("p (g r) -> p r g", r=PAGE)
 
-        key_scales = gather_scales("key_scales", key_scale_pool)
-        val_scales = gather_scales("val_scales", val_scale_pool)
-        q_codes, q_scales = quantise("q", [q_raw, dq_raw])
-        table = load_plain("table", ptab, TABLE, "stage_a", nc.sync)
-        val_pool = load_words("val_pool", vals_words, "stage_b")
+        q_codes, q_scales = quantise("q", [q_raw, dq_raw], nc.vector.tensor_copy)
         floors = sb.tile([P, PAGES], F32, name="floors", tag="floors", align_bytes=64)
         nc.vector.tensor_copy(floors[:], table[:].indirect(pages[:]))
-        go_raw = load_rows("go_raw", gout, "stage_a", nc.sync)
+        go_raw = load_rows("go_raw", gout, "stage_a", nc.scalar)
 
+        key_scales = gather_scales("key_scales", key_scale_pool)
+        val_scales = gather_scales("val_scales", val_scale_pool)
+        key_words = sb.tile([P, SLOTS], U32, name="key_words", tag="val_scale_pool", align_bytes=64)
+        val_words = sb.tile([P, SLOTS], U32, name="val_words", align_bytes=64)
         score, dscore = [], []
         for half in range(HALVES):
-            keys = gather_words("keys%d" % half, key_pool, half)
+            keys = gather_words(key_words, key_pool, half)
             score.append(product("a%d" % half, q_codes, q_scales, 0, keys, key_scales, 0, half))
             dscore.append(product("t%d" % half, q_codes, q_scales, P, keys, key_scales, 0, half))
+
+        go_codes, go_scales = quantise("go", [go_raw], nc.scalar.copy)
 
         def wide(name):
             return sb.tile([P, PAGE, PAGES], F32, name=name)
@@ -139,18 +145,15 @@ def tile_attend_hvpagefloor_kernel(tc, query, keys_words, keys_scales, ptab, res
             nc.vector.scalar_tensor_tensor(y[:, :, g], floors[:, g].unsqueeze(1).to_broadcast([P, PAGE, HALF_PAGES]),
                                            lam_col[:], score[half], ALU.mult, ALU.subtract)
             nc.scalar.activation(rest[:, :, g], y[:, :, g], ACT.Sigmoid)
-        reserve_col = load_plain("reserve_col", reserve, 1, "col", nc.sync)
-        base_t = load_plain("base_t", base, PAGES, "floors", nc.sync)
         for half in range(HALVES):
             g = part(half)
             nc.vector.scalar_tensor_tensor(neg_xp[:, :, g], rest[:, :, g], 1.0, dscore[half], ALU.subtract, ALU.mult,
                                            accum_out=neg_xz[half][:])
         nc.scalar.activation(log_rest[:], rest, ACT.Ln, bias=ln_floor[:])
 
-        go_codes, go_scales = quantise("go", [go_raw])
         c0 = []
         for half in range(HALVES):
-            vals = gather_words("vals%d" % half, val_pool, half)
+            vals = gather_words(val_words, val_pool, half)
             c0.append(product("c%d" % half, go_codes, go_scales, 0, vals, val_scales, VALS_ROW, half))
 
         neg_sum_p, z, inv_z, alpha, c1, c2 = (col(n) for n in ("neg_sum_p", "z", "inv_z", "alpha", "c1", "c2"))

@@ -23,8 +23,7 @@ TABLE = 512
 BANK = 512
 HALVES = SLOTS // BANK
 HALF_PAGES = PAGES // HALVES
-VALS_ROW = 4
-LN_FLOOR = 2.0 ** -40
+LOGIT_FLOOR = -28.0
 GAIN = 64.0
 
 FLOPS = 3 * 2 * 512 * P * SLOTS
@@ -37,98 +36,54 @@ def tile_attend_hvpagefloor_kernel(tc, query, keys_words, keys_scales, ptab, res
         sb = ctx.enter_context(tc.tile_pool(name="sb", bufs=1))
         ps = ctx.enter_context(tc.psum_pool(name="ps", bufs=1))
 
-        slots = sb.tile([P, SLOTS // 16], U16, name="slots")
-        pages = sb.tile([P, PAGES // 16], U16, name="pages")
-        nc.sync.dma_start(slots[:], offs)
-
-        def load_scales(name, src, row, queue):
+        def load_scales(name, src):
             window = sb.tile([P, TOKENS], U8, name=name, align_bytes=64)
             nc.vector.memset(window[:].bitcast(I32), 0)
-            for quad in range(4):
-                queue.dma_start(window[32 * quad + row:32 * quad + row + 4, :].bitcast(I32),
-                                src[0, 4 * quad:4 * quad + 4, :].bitcast(I32))
+            nc.sync.dma_start(window[0:P:8, :].bitcast(I32), src[0].bitcast(I32))
             return window
 
-        def load_words(name, src, tag):
-            window = sb.tile([P, TOKENS], I32, name=name, tag=tag, align_bytes=64)
+        def gather_scales(name, window):
+            picked = sb.tile([P, SLOTS], U8, name=name + "_picked", align_bytes=64)
+            nc.vector.tensor_copy(picked[:], window[:].indirect(slots[:]))
+            plane = sb.tile([P, SLOTS], U8, name=name, align_bytes=64)
+            nc.vector.memset(plane[:].bitcast(I32), 0)
+            for r in range(4):
+                nc.sync.dma_start(plane[r:P:32, :].bitcast(I32), picked[8 * r:P:32, :].bitcast(I32))
+            return plane
+
+        def load_words(name, src):
+            window = sb.tile([P, TOKENS], I32, name=name, align_bytes=64)
             nc.sync.dma_start(window[:], src[0].rearrange("p n t -> p (n t)").bitcast(I32))
             return window
 
-        def load_rows(name, src, tag, queue):
-            raw = sb.tile([P, PACK, P], F32, name=name, tag=tag, align_bytes=64)
-            queue.dma_start(raw[:], src.rearrange("(p j) w -> p j w", j=PACK))
+        def load_rows(name, src):
+            raw = sb.tile([P, PACK, P], F32, name=name)
+            nc.sync.dma_start(raw[:], src.rearrange("(p j) w -> p j w", j=PACK))
             return raw
 
-        def load_plain(name, src, width, tag, queue):
-            tile = sb.tile([P, width], F32, name=name, tag=tag, align_bytes=64)
-            queue.dma_start(tile[:], src)
+        def load_plain(name, src, width, dtype=F32):
+            tile = sb.tile([P, width], dtype, name=name)
+            nc.sync.dma_start(tile[:], src)
             return tile
 
-        nc.sync.dma_start(pages[:], offs2)
-        lam_col = load_plain("lam_col", lam, 1, "lam_col", nc.scalar)
-        key_scale_pool = load_scales("key_scale_pool", keys_scales, 0, nc.scalar)
-        val_scale_pool = load_scales("val_scale_pool", vals_scales, VALS_ROW, nc.scalar)
-        q_raw = load_rows("q_raw", query, "stage_a", nc.sync)
-        dq_raw = load_rows("dq_raw", dquery, "dq_raw", nc.sync)
-        table = load_plain("table", ptab, TABLE, "table", nc.sync)
-        key_pool = load_words("key_pool", keys_words, "key_pool")
-        val_pool = load_words("val_pool", vals_words, "val_pool")
-        reserve_col = load_plain("reserve_col", reserve, 1, "reserve_col", nc.sync)
-        base_t = load_plain("base_t", base, PAGES, "base_t", nc.sync)
-
-        ident = sb.tile([P, P], F32, name="ident")
-        make_identity(nc, ident[:])
-        ln_floor = sb.tile([P, 1], F32, name="ln_floor")
-        nc.gpsimd.memset(ln_floor[:], LN_FLOOR)
-
-        def quantise(name, raws, copy):
-            width = P * len(raws)
-            grouped = sb.tile([P, width, PACK], BF16, name=name + "_bf16", align_bytes=64)
-            for n, raw in enumerate(raws):
-                copy(grouped[:, n * P:(n + 1) * P, :], raw[:].rearrange("p j w -> p w j"))
-            codes = sb.tile([P, width], U32, name=name + "_codes", align_bytes=64)
-            scales = sb.tile([P, width], U8, name=name + "_scales", align_bytes=64)
-            nc.vector.quantize_mx(out=codes[:].bitcast(FP8X4), scales=scales[:],
-                                  in_=grouped[:].rearrange("p w j -> p (w j)"))
-            return codes, scales
-
-        def gather_scales(name, window):
-            picked = sb.tile([P, SLOTS], U8, name=name, align_bytes=64)
-            nc.vector.tensor_copy(picked[:], window[:].indirect(slots[:]))
-            return picked
-
-        def gather_words(picked, window, half):
-            cols = BANK // 16
-            words = picked[:, half * BANK:(half + 1) * BANK]
-            nc.vector.tensor_copy(words, window[:].bitcast(U32).indirect(slots[:, half * cols:(half + 1) * cols]))
-            return words
-
-        def product(tag, codes, scales, col, words, word_scales, row, half):
-            bank = ps.tile([P, BANK], F32, name=tag, tag=tag)
-            nc.tensor.matmul_mx(out=bank[:], lhsT=codes[:, col:col + P].bitcast(FP8X4), lhsT_scale=scales[:, col:col + P],
-                                rhs=words.bitcast(FP8X4), rhs_scale=word_scales[row:P, half * BANK:(half + 1) * BANK],
-                                start=True, stop=True)
-            return bank[:].rearrange("p (g r) -> p r g", r=PAGE)
-
-        q_codes, q_scales = quantise("q", [q_raw, dq_raw], nc.vector.tensor_copy)
-        floors = sb.tile([P, PAGES], F32, name="floors", tag="floors", align_bytes=64)
-        nc.vector.tensor_copy(floors[:], table[:].indirect(pages[:]))
-        go_raw = load_rows("go_raw", gout, "stage_a", nc.scalar)
-
+        slots = load_plain("slots", offs, SLOTS // 16, U16)
+        pages = load_plain("pages", offs2, PAGES // 16, U16)
+        lam_col = load_plain("lam_col", lam, 1)
+        q_raw = load_rows("q_raw", query)
+        key_scale_pool = load_scales("key_scale_pool", keys_scales)
+        val_scale_pool = load_scales("val_scale_pool", vals_scales)
+        key_pool = load_words("key_pool", keys_words)
+        dq_raw = load_rows("dq_raw", dquery)
+        table = load_plain("table", ptab, TABLE)
         key_scales = gather_scales("key_scales", key_scale_pool)
+        val_pool = load_words("val_pool", vals_words)
         val_scales = gather_scales("val_scales", val_scale_pool)
-        key_words = sb.tile([P, SLOTS], U32, name="key_words", tag="val_scale_pool", align_bytes=64)
-        val_words = sb.tile([P, SLOTS], U32, name="val_words", align_bytes=64)
-        score, dscore = [], []
-        for half in range(HALVES):
-            keys = gather_words(key_words, key_pool, half)
-            score.append(product("a%d" % half, q_codes, q_scales, 0, keys, key_scales, 0, half))
-            dscore.append(product("t%d" % half, q_codes, q_scales, P, keys, key_scales, 0, half))
+        go_raw = load_rows("go_raw", gout)
+        reserve_col = load_plain("reserve_col", reserve, 1)
+        base_t = load_plain("base_t", base, PAGES)
 
-        go_codes, go_scales = quantise("go", [go_raw], nc.scalar.copy)
-
-        def wide(name):
-            return sb.tile([P, PAGE, PAGES], F32, name=name)
+        def wide(name, **kw):
+            return sb.tile([P, PAGE, PAGES], F32, name=name, **kw)
 
         def col(name, width=1):
             return sb.tile([P, width], F32, name=name)
@@ -136,9 +91,61 @@ def tile_attend_hvpagefloor_kernel(tc, query, keys_words, keys_scales, ptab, res
         def part(half):
             return slice(half * HALF_PAGES, (half + 1) * HALF_PAGES)
 
-        y, log_rest, neg_p, neg_xp, w = wide("y"), wide("log_rest"), wide("neg_p"), wide("neg_xp"), wide("w")
-        pair = sb.tile([P, PAGE, 2, PAGES], F32, name="pair")
-        rest, n_term = pair[:, :, 0, :], pair[:, :, 1, :]
+        logit_floor, ln_floor = col("logit_floor"), col("ln_floor")
+        nc.vector.memset(logit_floor[:], LOGIT_FLOOR)
+        nc.scalar.activation(ln_floor[:], logit_floor[:], ACT.Sigmoid)
+        ident = sb.tile([P, P], F32, name="ident")
+        make_identity(nc, ident[:])
+
+        def quantise(name, raw):
+            grouped = sb.tile([P, P, PACK], BF16, name=name + "_bf16", tag=name + "_bf16", align_bytes=64)
+            nc.scalar.copy(grouped[:], raw[:].rearrange("p j w -> p w j"))
+            codes = sb.tile([P, P], U32, name=name + "_codes", align_bytes=64)
+            scales = sb.tile([P, P], U8, name=name + "_scales", align_bytes=64)
+            nc.vector.quantize_mx(out=codes[:].bitcast(FP8X4), scales=scales[:],
+                                  in_=grouped[:].rearrange("p w j -> p (w j)"))
+            return codes, scales
+
+        def gather_words(name, window, half):
+            cols = BANK // 16
+            words = sb.tile([P, BANK], U32, name=name, align_bytes=64)
+            nc.vector.tensor_copy(words[:], window[:].bitcast(U32).indirect(slots[:, half * cols:(half + 1) * cols]))
+            return words
+
+        def product(tag, rows, words, word_scales, half):
+            bank = ps.tile([P, BANK], F32, name=tag, tag=tag)
+            nc.tensor.matmul_mx(out=bank[:], lhsT=rows[0][:].bitcast(FP8X4), lhsT_scale=rows[1][:],
+                                rhs=words[:].bitcast(FP8X4), rhs_scale=word_scales[:, half * BANK:(half + 1) * BANK],
+                                start=True, stop=True)
+            return bank[:].rearrange("p (g r) -> p r g", r=PAGE)
+
+        def page_sums(name, values, tags):
+            turned = ps.tile([P, P], F32, name=name + "_turned", tag=tags[0])
+            for r in range(0, PAGE, 2):
+                nc.tensor.matmul(turned[:], lhsT=values[:, r:r + 2, :].rearrange("p a g -> p (a g)"), rhs=ident[:],
+                                 is_transpose=True, start=(r == 0), stop=(r == PAGE - 2))
+            staged = sb.tile([P, P], F32, name=name + "_staged")
+            nc.scalar.copy(staged[:], turned[:])
+            back = ps.tile([P, P], F32, name=name + "_back", tag=tags[1])
+            nc.tensor.transpose(back[:], staged[:], ident[:])
+            return back
+
+        def folded(name, back):
+            both = col(name + "_both", P)
+            nc.scalar.copy(both[:], back[:])
+            total = col(name + "_total", PAGES)
+            nc.gpsimd.tensor_tensor(total[:], both[:, 0:PAGES], both[:, PAGES:P], ALU.add)
+            return total
+
+        q_mx = quantise("q", q_raw)
+        keys = [gather_words("keys%d" % half, key_pool, half) for half in range(HALVES)]
+        score = [product("a%d" % half, q_mx, keys[half], key_scales, half) for half in range(HALVES)]
+        dq_mx = quantise("dq", dq_raw)
+        dscore = [product("t%d" % half, dq_mx, keys[half], key_scales, half) for half in range(HALVES)]
+        floors = col("floors", PAGES)
+        nc.vector.tensor_copy(floors[:], table[:].indirect(pages[:]))
+
+        y, rest, log_rest, neg_xp, w = (wide(n) for n in ("y", "rest", "log_rest", "neg_xp", "w"))
         neg_xz = [col("neg_xz%d" % h) for h in range(HALVES)]
         for half in range(HALVES):
             g = part(half)
@@ -149,58 +156,59 @@ def tile_attend_hvpagefloor_kernel(tc, query, keys_words, keys_scales, ptab, res
             g = part(half)
             nc.vector.scalar_tensor_tensor(neg_xp[:, :, g], rest[:, :, g], 1.0, dscore[half], ALU.subtract, ALU.mult,
                                            accum_out=neg_xz[half][:])
-        nc.scalar.activation(log_rest[:], rest, ACT.Ln, bias=ln_floor[:])
-
-        c0 = []
         for half in range(HALVES):
-            vals = gather_words(val_words, val_pool, half)
-            c0.append(product("c%d" % half, go_codes, go_scales, 0, vals, val_scales, VALS_ROW, half))
+            r = slice(half * PAGE // 2, (half + 1) * PAGE // 2)
+            nc.scalar.activation(log_rest[:, r, :], rest[:, r, :], ACT.Ln, bias=ln_floor[:])
+        rest_sums = folded("rest", page_sums("rest", rest, ("f", "g")))
 
-        neg_sum_p, z, inv_z, alpha, c1, c2 = (col(n) for n in ("neg_sum_p", "z", "inv_z", "alpha", "c1", "c2"))
-        nc.vector.scalar_tensor_tensor(neg_p[:], y[:], 1.0, log_rest[:], ALU.mult, ALU.min, accum_out=neg_sum_p[:])
-        nc.vector.tensor_tensor(z[:], reserve_col[:], neg_sum_p[:], ALU.subtract)
+        vals = [gather_words("vals%d" % half, val_pool, half) for half in range(HALVES)]
+        go_mx = quantise("go", go_raw)
+        c0 = [product("c%d" % half, go_mx, vals[half], val_scales, half) for half in range(HALVES)]
+
+        neg_p = wide("neg_p", tag="val_pool", align_bytes=64)
+        z, inv_z, alpha, c1, c2 = (col(n) for n in ("z", "inv_z", "alpha", "c1", "c2"))
+        neg_sum_p = [col("neg_sum_p%d" % h) for h in range(HALVES)]
+        for half in range(HALVES):
+            r = slice(half * PAGE // 2, (half + 1) * PAGE // 2)
+            nc.vector.scalar_tensor_tensor(neg_p[:, r, :], y[:, r, :], 1.0, log_rest[:, r, :], ALU.mult, ALU.min,
+                                           accum_out=neg_sum_p[half][:])
+        nc.vector.tensor_scalar(z[:], reserve_col[:], neg_sum_p[0][:], neg_sum_p[1][:], ALU.subtract, ALU.subtract)
+        n_term = wide("n_term", tag="go_bf16", align_bytes=64)
         nc.vector.reciprocal(inv_z[:], z[:])
         nc.vector.tensor_scalar(alpha[:], neg_xz[0][:], neg_xz[1][:], inv_z[:], ALU.add, ALU.mult)
         nc.scalar.activation(c1[:], inv_z[:], ACT.Square, scale=8.0)
         nc.scalar.activation(c2[:], inv_z[:], ACT.Copy, scale=GAIN)
-        nc.vector.scalar_tensor_tensor(n_term, neg_xp[:], alpha[:], rest, ALU.add, ALU.mult)
-
-        def page_sums(name, blocks, tags):
-            turned = ps.tile([P, P], F32, name=name + "_turned", tag=tags[0])
-            for n, block in enumerate(blocks):
-                nc.tensor.matmul(turned[:], lhsT=block, rhs=ident[:], is_transpose=True,
-                                 start=(n == 0), stop=(n == len(blocks) - 1))
-            staged = sb.tile([P, P], F32, name=name + "_staged")
-            nc.scalar.copy(staged[:], turned[:])
-            back = ps.tile([P, P], F32, name=name + "_back", tag=tags[1])
-            nc.tensor.transpose(back[:], staged[:], ident[:])
-            return back
-
+        nc.vector.scalar_tensor_tensor(n_term[:], neg_xp[:], alpha[:], rest[:], ALU.add, ALU.mult)
         for half in range(HALVES):
             g = part(half)
             nc.vector.scalar_tensor_tensor(w[:, :, g], n_term[:, :, g], alpha[:], c0[half], ALU.subtract, ALU.mult)
-        pair_sums = page_sums("pair", [pair[:, r, :, :].rearrange("p a g -> p (a g)") for r in range(PAGE)], ("f", "g"))
-        w_sums = page_sums("w", [w[:, r:r + 2, :].rearrange("p a g -> p (a g)") for r in range(0, PAGE, 2)], ("a0", "a1"))
+        n_sums = folded("n", page_sums("n", n_term, ("t0", "t1")))
+        w_sums = page_sums("w", w, ("a0", "a1"))
 
-        e1, rest32, e2 = (col(n, PAGES) for n in ("e1", "rest32", "e2"))
-        nc.scalar.activation(e1[:], pair_sums[:, 0:PAGES], ACT.Copy, bias=-float(PAGE))
-        nc.scalar.activation(rest32[:], pair_sums[:, 0:PAGES], ACT.Copy, bias=-2.0 * PAGE)
+        e1, e2_rest, e2 = (col(n, PAGES) for n in ("e1", "e2_rest", "e2"))
+        nc.gpsimd.tensor_scalar(e1[:], rest_sums[:], -float(PAGE), 1.0, ALU.add, ALU.mult)
+        nc.gpsimd.tensor_scalar(e2_rest[:], rest_sums[:], -2.0 * PAGE, alpha[:], ALU.add, ALU.mult)
+        nc.gpsimd.tensor_tensor(e2[:], e2_rest[:], n_sums[:], ALU.add)
 
-        dots = {}
-        for name, factor in (("b", neg_xp), ("a", neg_p)):
-            for half in range(HALVES):
-                g = part(half)
-                unused = sb.tile([P, PAGE, HALF_PAGES], F32, name="unused_%s%d" % (name, half))
-                dots[name, half] = col("dot_%s%d" % (name, half))
-                nc.vector.scalar_tensor_tensor(unused[:], factor[:, :, g], c1[:], c0[half], ALU.mult, ALU.mult,
-                                               accum_out=dots[name, half][:])
+        def dot(name, factor, half):
+            unused = sb.tile([P, PAGE, HALF_PAGES], F32, name="unused_" + name)
+            total = col("dot_" + name)
+            nc.vector.scalar_tensor_tensor(unused[:], factor[:, :, part(half)], c1[:], c0[half], ALU.mult, ALU.mult,
+                                           accum_out=total[:])
+            return total
 
-        nc.vector.scalar_tensor_tensor(e2[:], rest32[:], alpha[:], pair_sums[:, PAGES:P], ALU.mult, ALU.add)
-        terms = [(e1[:], dots["b", 0]), (e1[:], dots["b", 1]), (w_sums[:, 0:PAGES], c2), (w_sums[:, PAGES:P], c2),
-                 (e2[:], dots["a", 0]), (e2[:], dots["a", 1])]
-        total = base_t
-        for n, (term, factor) in enumerate(terms):
-            nxt = col("total%d" % n, PAGES)
-            nc.vector.scalar_tensor_tensor(nxt[:], term, factor[:], total[:], ALU.mult, ALU.add)
-            total = nxt
+        def add_term(name, total, term, factor):
+            result = col(name, PAGES)
+            nc.vector.scalar_tensor_tensor(result[:], term, factor[:], total[:], ALU.mult, ALU.add)
+            return result
+
+        dot_b = [dot("b%d" % half, neg_xp, half) for half in range(HALVES)]
+        total = add_term("with_b0", base_t, e1[:], dot_b[0])
+        dot_a0 = dot("a0", neg_p, 0)
+        total = add_term("with_b1", total, e1[:], dot_b[1])
+        total = add_term("with_w0", total, w_sums[:, 0:PAGES], c2)
+        dot_a1 = dot("a1", neg_p, 1)
+        total = add_term("with_w1", total, w_sums[:, PAGES:P], c2)
+        total = add_term("with_a0", total, e2[:], dot_a0)
+        total = add_term("with_a1", total, e2[:], dot_a1)
         nc.sync.dma_start(out, total[:])

@@ -71,14 +71,14 @@ def tile_attend_hvpagefloor_kernel(tc, query, keys_words, keys_scales, ptab, res
         lam_col = load_plain("lam_col", lam, 1)
         q_raw = load_rows("q_raw", query)
         key_scale_pool = load_scales("key_scale_pool", keys_scales)
+        dq_raw = load_rows("dq_raw", dquery)
         val_scale_pool = load_scales("val_scale_pool", vals_scales)
         key_pool = load_words("key_pool", keys_words)
-        dq_raw = load_rows("dq_raw", dquery)
         table = load_plain("table", ptab, TABLE)
         key_scales = gather_scales("key_scales", key_scale_pool)
         val_pool = load_words("val_pool", vals_words)
-        val_scales = gather_scales("val_scales", val_scale_pool)
         go_raw = load_rows("go_raw", gout)
+        val_scales = gather_scales("val_scales", val_scale_pool)
         reserve_col = load_plain("reserve_col", reserve, 1)
         base_t = load_plain("base_t", base, PAGES)
 
@@ -95,16 +95,19 @@ def tile_attend_hvpagefloor_kernel(tc, query, keys_words, keys_scales, ptab, res
         nc.vector.memset(logit_floor[:], LOGIT_FLOOR)
         nc.scalar.activation(ln_floor[:], logit_floor[:], ACT.Sigmoid)
         ident = sb.tile([P, P], F32, name="ident")
-        make_identity(nc, ident[:])
+        nc.vector.memset(ident[:], 0.0)
+        make_identity(nc, ident[:], nomemset=True)
 
-        def quantise(name, raw):
-            grouped = sb.tile([P, P, PACK], BF16, name=name + "_bf16", tag=name + "_bf16", align_bytes=64)
-            nc.scalar.copy(grouped[:], raw[:].rearrange("p j w -> p w j"))
-            codes = sb.tile([P, P], U32, name=name + "_codes", align_bytes=64)
-            scales = sb.tile([P, P], U8, name=name + "_scales", align_bytes=64)
+        def quantise(name, raws):
+            width = P * len(raws)
+            grouped = sb.tile([P, width, PACK], BF16, name=name + "_bf16", tag=name + "_bf16", align_bytes=64)
+            for n, raw in enumerate(raws):
+                nc.scalar.copy(grouped[:, n * P:(n + 1) * P, :], raw[:].rearrange("p j w -> p w j"))
+            codes = sb.tile([P, width], U32, name=name + "_codes", align_bytes=64)
+            scales = sb.tile([P, width], U8, name=name + "_scales", align_bytes=64)
             nc.vector.quantize_mx(out=codes[:].bitcast(FP8X4), scales=scales[:],
                                   in_=grouped[:].rearrange("p w j -> p (w j)"))
-            return codes, scales
+            return [(codes[:, n * P:(n + 1) * P], scales[:, n * P:(n + 1) * P]) for n in range(len(raws))]
 
         def gather_words(name, window, half):
             cols = BANK // 16
@@ -114,7 +117,7 @@ def tile_attend_hvpagefloor_kernel(tc, query, keys_words, keys_scales, ptab, res
 
         def product(tag, rows, words, word_scales, half):
             bank = ps.tile([P, BANK], F32, name=tag, tag=tag)
-            nc.tensor.matmul_mx(out=bank[:], lhsT=rows[0][:].bitcast(FP8X4), lhsT_scale=rows[1][:],
+            nc.tensor.matmul_mx(out=bank[:], lhsT=rows[0].bitcast(FP8X4), lhsT_scale=rows[1],
                                 rhs=words[:].bitcast(FP8X4), rhs_scale=word_scales[:, half * BANK:(half + 1) * BANK],
                                 start=True, stop=True)
             return bank[:].rearrange("p (g r) -> p r g", r=PAGE)
@@ -137,10 +140,9 @@ def tile_attend_hvpagefloor_kernel(tc, query, keys_words, keys_scales, ptab, res
             nc.gpsimd.tensor_tensor(total[:], both[:, 0:PAGES], both[:, PAGES:P], ALU.add)
             return total
 
-        q_mx = quantise("q", q_raw)
+        q_mx, dq_mx = quantise("q", [q_raw, dq_raw])
         keys = [gather_words("keys%d" % half, key_pool, half) for half in range(HALVES)]
         score = [product("a%d" % half, q_mx, keys[half], key_scales, half) for half in range(HALVES)]
-        dq_mx = quantise("dq", dq_raw)
         dscore = [product("t%d" % half, dq_mx, keys[half], key_scales, half) for half in range(HALVES)]
         floors = col("floors", PAGES)
         nc.vector.tensor_copy(floors[:], table[:].indirect(pages[:]))
@@ -156,29 +158,27 @@ def tile_attend_hvpagefloor_kernel(tc, query, keys_words, keys_scales, ptab, res
             g = part(half)
             nc.vector.scalar_tensor_tensor(neg_xp[:, :, g], rest[:, :, g], 1.0, dscore[half], ALU.subtract, ALU.mult,
                                            accum_out=neg_xz[half][:])
-        for half in range(HALVES):
-            r = slice(half * PAGE // 2, (half + 1) * PAGE // 2)
-            nc.scalar.activation(log_rest[:, r, :], rest[:, r, :], ACT.Ln, bias=ln_floor[:])
+        nc.scalar.activation(log_rest[:], rest[:], ACT.Ln, bias=ln_floor[:])
         rest_sums = folded("rest", page_sums("rest", rest, ("f", "g")))
 
         vals = [gather_words("vals%d" % half, val_pool, half) for half in range(HALVES)]
-        go_mx = quantise("go", go_raw)
+        go_mx, = quantise("go", [go_raw])
         c0 = [product("c%d" % half, go_mx, vals[half], val_scales, half) for half in range(HALVES)]
+        c0_first = sb.tile([P, PAGE, HALF_PAGES], F32, name="c0_first")
+        nc.scalar.copy(c0_first[:], c0[0])
 
         neg_p = wide("neg_p", tag="val_pool", align_bytes=64)
         z, inv_z, alpha, c1, c2 = (col(n) for n in ("z", "inv_z", "alpha", "c1", "c2"))
-        neg_sum_p = [col("neg_sum_p%d" % h) for h in range(HALVES)]
-        for half in range(HALVES):
-            r = slice(half * PAGE // 2, (half + 1) * PAGE // 2)
-            nc.vector.scalar_tensor_tensor(neg_p[:, r, :], y[:, r, :], 1.0, log_rest[:, r, :], ALU.mult, ALU.min,
-                                           accum_out=neg_sum_p[half][:])
-        nc.vector.tensor_scalar(z[:], reserve_col[:], neg_sum_p[0][:], neg_sum_p[1][:], ALU.subtract, ALU.subtract)
+        neg_sum_p = col("neg_sum_p")
+        nc.vector.scalar_tensor_tensor(neg_p[:], y[:], 1.0, log_rest[:], ALU.mult, ALU.min, accum_out=neg_sum_p[:])
+        nc.vector.tensor_tensor(z[:], reserve_col[:], neg_sum_p[:], ALU.subtract)
         n_term = wide("n_term", tag="go_bf16", align_bytes=64)
         nc.vector.reciprocal(inv_z[:], z[:])
         nc.vector.tensor_scalar(alpha[:], neg_xz[0][:], neg_xz[1][:], inv_z[:], ALU.add, ALU.mult)
         nc.scalar.activation(c1[:], inv_z[:], ACT.Square, scale=8.0)
         nc.scalar.activation(c2[:], inv_z[:], ACT.Copy, scale=GAIN)
-        nc.vector.scalar_tensor_tensor(n_term[:], neg_xp[:], alpha[:], rest[:], ALU.add, ALU.mult)
+        for r in (slice(0, PAGE // 2), slice(PAGE // 2, PAGE)):
+            nc.vector.scalar_tensor_tensor(n_term[:, r, :], neg_xp[:, r, :], alpha[:], rest[:, r, :], ALU.add, ALU.mult)
         for half in range(HALVES):
             g = part(half)
             nc.vector.scalar_tensor_tensor(w[:, :, g], n_term[:, :, g], alpha[:], c0[half], ALU.subtract, ALU.mult)
@@ -202,13 +202,18 @@ def tile_attend_hvpagefloor_kernel(tc, query, keys_words, keys_scales, ptab, res
             nc.vector.scalar_tensor_tensor(result[:], term, factor[:], total[:], ALU.mult, ALU.add)
             return result
 
+        a_products = sb.tile([P, PAGE, HALF_PAGES], F32, name="a_products", tag="rest")
+        nc.gpsimd.tensor_tensor(a_products[:], neg_p[:, :, part(0)], c0_first[:], ALU.mult)
+        unused_a0 = sb.tile([P, PAGE, HALF_PAGES], F32, name="unused_a0", tag="n_staged")
+        dot_a0 = col("dot_a0")
+        nc.scalar.activation(unused_a0[:], a_products[:], ACT.Copy, scale=c1[:], accum_out=dot_a0[:])
         dot_b = [dot("b%d" % half, neg_xp, half) for half in range(HALVES)]
         total = add_term("with_b0", base_t, e1[:], dot_b[0])
-        dot_a0 = dot("a0", neg_p, 0)
-        total = add_term("with_b1", total, e1[:], dot_b[1])
-        total = add_term("with_w0", total, w_sums[:, 0:PAGES], c2)
         dot_a1 = dot("a1", neg_p, 1)
+        total = add_term("with_b1", total, e1[:], dot_b[1])
+        dot_a = col("dot_a")
+        nc.vector.tensor_tensor(dot_a[:], dot_a0[:], dot_a1[:], ALU.add)
+        total = add_term("with_a", total, e2[:], dot_a)
+        total = add_term("with_w0", total, w_sums[:, 0:PAGES], c2)
         total = add_term("with_w1", total, w_sums[:, PAGES:P], c2)
-        total = add_term("with_a0", total, e2[:], dot_a0)
-        total = add_term("with_a1", total, e2[:], dot_a1)
         nc.sync.dma_start(out, total[:])

from contextlib import ExitStack

import concourse.mybir as mybir
from concourse.masks import make_identity

F32 = mybir.dt.float32
BF16 = mybir.dt.bfloat16
I32 = mybir.dt.int32
U32 = mybir.dt.uint32
U16 = mybir.dt.uint16
U8 = mybir.dt.uint8
FP8X4 = mybir.dt.float8_e4m3fn_x4
ALU = mybir.AluOpType
ACT = mybir.ActivationFunctionType

P = 128
PACK = 4
TOKENS = 4096
SLOTS = 1024
PAGES = 64
PAGE = 16
TABLE = 512
BANK = 512
HALVES = SLOTS // BANK
HALF_PAGES = PAGES // HALVES
LOGIT_FLOOR = -28.0
GAIN = 64.0

FLOPS = 3 * 2 * 512 * P * SLOTS


def tile_attend_hvpagefloor_kernel(tc, query, keys_words, keys_scales, ptab, reserve, gout, vals_words, vals_scales,
                                    lam, dquery, base, offs, offs2, out):
    nc = tc.nc
    with ExitStack() as ctx:
        sb = ctx.enter_context(tc.tile_pool(name="sb", bufs=1))
        ps = ctx.enter_context(tc.psum_pool(name="ps", bufs=1))

        def load_scales(name, src):
            window = sb.tile([P, TOKENS], U8, name=name, align_bytes=64)
            nc.vector.memset(window[:].bitcast(I32), 0)
            nc.sync.dma_start(window[0:P:8, :].bitcast(I32), src[0].bitcast(I32))
            return window

        def gather_scales(name, window):
            picked = sb.tile([P, SLOTS], U8, name=name + "_picked", align_bytes=64)
            nc.vector.tensor_copy(picked[:], window[:].indirect(slots[:]))
            plane = sb.tile([P, SLOTS], U8, name=name, align_bytes=64)
            nc.vector.memset(plane[:].bitcast(I32), 0)
            for r in range(4):
                nc.sync.dma_start(plane[r:P:32, :].bitcast(I32), picked[8 * r:P:32, :].bitcast(I32))
            return plane

        def load_words(name, src):
            window = sb.tile([P, TOKENS], I32, name=name, align_bytes=64)
            nc.sync.dma_start(window[:], src[0].rearrange("p n t -> p (n t)").bitcast(I32))
            return window

        def load_rows(name, src):
            raw = sb.tile([P, PACK, P], F32, name=name)
            nc.sync.dma_start(raw[:], src.rearrange("(p j) w -> p j w", j=PACK))
            return raw

        def load_plain(name, src, width, dtype=F32):
            tile = sb.tile([P, width], dtype, name=name)
            nc.sync.dma_start(tile[:], src)
            return tile

        slots = load_plain("slots", offs, SLOTS // 16, U16)
        pages = load_plain("pages", offs2, PAGES // 16, U16)
        lam_col = load_plain("lam_col", lam, 1)
        q_raw = load_rows("q_raw", query)
        key_scale_pool = load_scales("key_scale_pool", keys_scales)
        dq_raw = load_rows("dq_raw", dquery)
        val_scale_pool = load_scales("val_scale_pool", vals_scales)
        key_pool = load_words("key_pool", keys_words)
        table = load_plain("table", ptab, TABLE)
        key_scales = gather_scales("key_scales", key_scale_pool)
        val_pool = load_words("val_pool", vals_words)
        go_raw = load_rows("go_raw", gout)
        val_scales = gather_scales("val_scales", val_scale_pool)
        reserve_col = load_plain("reserve_col", reserve, 1)
        base_t = load_plain("base_t", base, PAGES)

        def wide(name, **kw):
            return sb.tile([P, PAGE, PAGES], F32, name=name, **kw)

        def col(name, width=1):
            return sb.tile([P, width], F32, name=name)

        def part(half):
            return slice(half * HALF_PAGES, (half + 1) * HALF_PAGES)

        logit_floor, ln_floor = col("logit_floor"), col("ln_floor")
        nc.vector.memset(logit_floor[:], LOGIT_FLOOR)
        nc.scalar.activation(ln_floor[:], logit_floor[:], ACT.Sigmoid)
        ident = sb.tile([P, P], F32, name="ident")
        nc.vector.memset(ident[:], 0.0)
        make_identity(nc, ident[:], nomemset=True)

        def quantise(name, raws):
            width = P * len(raws)
            grouped = sb.tile([P, width, PACK], BF16, name=name + "_bf16", tag=name + "_bf16", align_bytes=64)
            for n, raw in enumerate(raws):
                nc.scalar.copy(grouped[:, n * P:(n + 1) * P, :], raw[:].rearrange("p j w -> p w j"))
            codes = sb.tile([P, width], U32, name=name + "_codes", align_bytes=64)
            scales = sb.tile([P, width], U8, name=name + "_scales", align_bytes=64)
            nc.vector.quantize_mx(out=codes[:].bitcast(FP8X4), scales=scales[:],
                                  in_=grouped[:].rearrange("p w j -> p (w j)"))
            return [(codes[:, n * P:(n + 1) * P], scales[:, n * P:(n + 1) * P]) for n in range(len(raws))]

        def gather_words(name, window, half):
            cols = BANK // 16
            words = sb.tile([P, BANK], U32, name=name, align_bytes=64)
            nc.vector.tensor_copy(words[:], window[:].bitcast(U32).indirect(slots[:, half * cols:(half + 1) * cols]))
            return words

        def product(tag, rows, words, word_scales, half):
            bank = ps.tile([P, BANK], F32, name=tag, tag=tag)
            nc.tensor.matmul_mx(out=bank[:], lhsT=rows[0].bitcast(FP8X4), lhsT_scale=rows[1],
                                rhs=words[:].bitcast(FP8X4), rhs_scale=word_scales[:, half * BANK:(half + 1) * BANK],
                                start=True, stop=True)
            return bank[:].rearrange("p (g r) -> p r g", r=PAGE)

        def page_sums(name, values, tags):
            turned = ps.tile([P, P], F32, name=name + "_turned", tag=tags[0])
            for r in range(0, PAGE, 2):
                nc.tensor.matmul(turned[:], lhsT=values[:, r:r + 2, :].rearrange("p a g -> p (a g)"), rhs=ident[:],
                                 is_transpose=True, start=(r == 0), stop=(r == PAGE - 2))
            staged = sb.tile([P, P], F32, name=name + "_staged")
            nc.scalar.copy(staged[:], turned[:])
            back = ps.tile([P, P], F32, name=name + "_back", tag=tags[1])
            nc.tensor.transpose(back[:], staged[:], ident[:])
            return back

        def folded(name, back):
            both = col(name + "_both", P)
            nc.scalar.copy(both[:], back[:])
            total = col(name + "_total", PAGES)
            nc.gpsimd.tensor_tensor(total[:], both[:, 0:PAGES], both[:, PAGES:P], ALU.add)
            return total

        q_mx, dq_mx = quantise("q", [q_raw, dq_raw])
        keys = [gather_words("keys%d" % half, key_pool, half) for half in range(HALVES)]
        score = [product("a%d" % half, q_mx, keys[half], key_scales, half) for half in range(HALVES)]
        dscore = [product("t%d" % half, dq_mx, keys[half], key_scales, half) for half in range(HALVES)]
        floors = col("floors", PAGES)
        nc.vector.tensor_copy(floors[:], table[:].indirect(pages[:]))

        y, rest, log_rest, neg_xp, w = (wide(n) for n in ("y", "rest", "log_rest", "neg_xp", "w"))
        neg_xz = [col("neg_xz%d" % h) for h in range(HALVES)]
        for half in range(HALVES):
            g = part(half)
            nc.vector.scalar_tensor_tensor(y[:, :, g], floors[:, g].unsqueeze(1).to_broadcast([P, PAGE, HALF_PAGES]),
                                           lam_col[:], score[half], ALU.mult, ALU.subtract)
            nc.scalar.activation(rest[:, :, g], y[:, :, g], ACT.Sigmoid)
        for half in range(HALVES):
            g = part(half)
            nc.vector.scalar_tensor_tensor(neg_xp[:, :, g], rest[:, :, g], 1.0, dscore[half], ALU.subtract, ALU.mult,
                                           accum_out=neg_xz[half][:])
        nc.scalar.activation(log_rest[:], rest[:], ACT.Ln, bias=ln_floor[:])
        rest_sums = folded("rest", page_sums("rest", rest, ("f", "g")))

        vals = [gather_words("vals%d" % half, val_pool, half) for half in range(HALVES)]
        go_mx, = quantise("go", [go_raw])
        c0 = [product("c%d" % half, go_mx, vals[half], val_scales, half) for half in range(HALVES)]
        c0_first = sb.tile([P, PAGE, HALF_PAGES], F32, name="c0_first")
        nc.scalar.copy(c0_first[:], c0[0])

        neg_p = wide("neg_p", tag="val_pool", align_bytes=64)
        z, inv_z, alpha, c1, c2 = (col(n) for n in ("z", "inv_z", "alpha", "c1", "c2"))
        neg_sum_p = col("neg_sum_p")
        nc.vector.scalar_tensor_tensor(neg_p[:], y[:], 1.0, log_rest[:], ALU.mult, ALU.min, accum_out=neg_sum_p[:])
        nc.vector.tensor_tensor(z[:], reserve_col[:], neg_sum_p[:], ALU.subtract)
        n_term = wide("n_term", tag="go_bf16", align_bytes=64)
        nc.vector.reciprocal(inv_z[:], z[:])
        nc.vector.tensor_scalar(alpha[:], neg_xz[0][:], neg_xz[1][:], inv_z[:], ALU.add, ALU.mult)
        nc.scalar.activation(c1[:], inv_z[:], ACT.Square, scale=8.0)
        nc.scalar.activation(c2[:], inv_z[:], ACT.Copy, scale=GAIN)
        for r in (slice(0, PAGE // 2), slice(PAGE // 2, PAGE)):
            nc.vector.scalar_tensor_tensor(n_term[:, r, :], neg_xp[:, r, :], alpha[:], rest[:, r, :], ALU.add, ALU.mult)
        for half in range(HALVES):
            g = part(half)
            nc.vector.scalar_tensor_tensor(w[:, :, g], n_term[:, :, g], alpha[:], c0[half], ALU.subtract, ALU.mult)
        n_sums = folded("n", page_sums("n", n_term, ("t0", "t1")))
        w_sums = page_sums("w", w, ("a0", "a1"))

        e1, e2_rest, e2 = (col(n, PAGES) for n in ("e1", "e2_rest", "e2"))
        nc.gpsimd.tensor_scalar(e1[:], rest_sums[:], -float(PAGE), 1.0, ALU.add, ALU.mult)
        nc.gpsimd.tensor_scalar(e2_rest[:], rest_sums[:], -2.0 * PAGE, alpha[:], ALU.add, ALU.mult)
        nc.gpsimd.tensor_tensor(e2[:], e2_rest[:], n_sums[:], ALU.add)

        def dot(name, factor, half):
            unused = sb.tile([P, PAGE, HALF_PAGES], F32, name="unused_" + name)
            total = col("dot_" + name)
            nc.vector.scalar_tensor_tensor(unused[:], factor[:, :, part(half)], c1[:], c0[half], ALU.mult, ALU.mult,
                                           accum_out=total[:])
            return total

        def add_term(name, total, term, factor):
            result = col(name, PAGES)
            nc.vector.scalar_tensor_tensor(result[:], term, factor[:], total[:], ALU.mult, ALU.add)
            return result

        a_products = sb.tile([P, PAGE, HALF_PAGES], F32, name="a_products", tag="rest")
        nc.gpsimd.tensor_tensor(a_products[:], neg_p[:, :, part(0)], c0_first[:], ALU.mult)
        unused_a0 = sb.tile([P, PAGE, HALF_PAGES], F32, name="unused_a0", tag="n_staged")
        dot_a0 = col("dot_a0")
        nc.scalar.activation(unused_a0[:], a_products[:], ACT.Copy, scale=c1[:], accum_out=dot_a0[:])
        dot_b = [dot("b%d" % half, neg_xp, half) for half in range(HALVES)]
        total = add_term("with_b0", base_t, e1[:], dot_b[0])
        dot_a1 = dot("a1", neg_p, 1)
        total = add_term("with_b1", total, e1[:], dot_b[1])
        dot_a = col("dot_a")
        nc.vector.tensor_tensor(dot_a[:], dot_a0[:], dot_a1[:], ALU.add)
        total = add_term("with_a", total, e2[:], dot_a)
        total = add_term("with_w0", total, w_sums[:, 0:PAGES], c2)
        total = add_term("with_w1", total, w_sums[:, PAGES:P], c2)
        nc.sync.dma_start(out, total[:])
